import numpy as np
import ml_dtypes


def mxq(x, axis, fmt="e4m3"):
    dtype, down = {"e4m3": (ml_dtypes.float8_e4m3fn, 7), "e5m2": (ml_dtypes.float8_e5m2, 14)}[fmt]
    v = np.moveaxis(np.asarray(x, np.float32).astype(ml_dtypes.bfloat16).astype(np.float64), axis, -1)
    blocks = v.reshape(v.shape[:-1] + (-1, 32))
    amax = np.abs(blocks).max(-1, keepdims=True)
    byte = np.maximum(np.where(amax > 0, np.frexp(amax)[1] - 1 + 127, 0) - down, 1)
    scale = np.exp2(byte - 127.0)
    codes = (blocks / scale).astype(np.float32).astype(dtype).astype(np.float64)
    return np.moveaxis((codes * scale).reshape(v.shape), -1, axis)


WIDE = False


def mx_kscale(k):
    if not WIDE:
        return np.ones(k)
    levels = np.array([10, -10, 5, -5, 0])
    if k % 512:
        return np.exp2(np.random.permutation(np.resize(levels, k // 32))).repeat(32)
    a = np.empty((k // 512, 16))
    for p in range(k // 512):
        a[p, :8] = np.random.permutation(np.resize(levels, 8))
        for g in range(8):
            far = levels[np.abs(levels - a[p, g]) >= 10]
            a[p, g + 8] = far[np.random.randint(len(far))]
    return np.exp2(a.ravel()).repeat(32)


def f64(x):
    return np.asarray(x).astype(np.float64)


def striped(idx):
    return np.tile(idx.reshape(-1, 16).T, (8, 1)).astype(np.uint16)


def unstriped(offs):
    return offs[:16].T.reshape(-1).astype(np.int64)


def pack_weight(w):
    k, n = w.shape
    w = f64(np.asarray(w, np.float32).astype(ml_dtypes.bfloat16)).reshape(k // 32, 32, n)
    amax = np.abs(w).max(1)
    byte = np.clip(np.where(amax > 0, np.frexp(amax)[1] - 1 + 127 - 7, 1), 1, 254)
    scaled = (w * np.exp2(127.0 - byte)[:, None, :]).reshape(k, n).astype(np.float32)
    words = np.ascontiguousarray(scaled.reshape(k // 512, 128, 4, n).transpose(0, 1, 3, 2)).astype(ml_dtypes.float8_e4m3fn).view(np.uint8)
    return words, np.ascontiguousarray(byte.astype(np.uint8).reshape(k // 512, 16, n))


def unpack_weight(words, scales):
    g, p, n, _ = words.shape
    vals = np.ascontiguousarray(words).view(ml_dtypes.float8_e4m3fn).astype(np.float64) * np.repeat(np.exp2(scales.astype(np.float64) - 127.0), 8, axis=1)[..., None]
    return vals.transpose(0, 1, 3, 2).reshape(g * 512, n)


def relu(v):
    return np.maximum(v, 0.0)


K, T, S, N, U = 1024, 2048, 512, 256, 1024


def setup_inputs():
    n = np.random.standard_normal
    s = mx_kscale(K)[:, None]
    packed_xT = pack_weight(n((K, T)) * s)
    return {
        "x_words": packed_xT[0],
        "x_scales": packed_xT[1],
        "w1": (n((K, N)) / np.sqrt(K) / s).astype(np.float32),
        "w2": (n((K, N)) / np.sqrt(K) / s).astype(np.float32),
        "ms": (n((N, U))).astype(np.float32),
        "hs": (np.random.uniform(0.1, 2.0, (N, U))).astype(np.float32),
        "par": (n((N, S))).astype(np.float32),
        "offs": striped(np.random.permutation(T)[:S]),
        "slot": striped(np.random.permutation(U)[:S]),
    }


def reference(x_words, x_scales, w1, w2, ms, hs, par, offs, slot):
    msg = f64(ms)[:, unstriped(slot)]
    xq = unpack_weight(x_words, x_scales)[:, unstriped(offs)]
    yg = mxq(f64(w1), 0, "e4m3").T @ xq
    mnew = 0.8 * msg + 0.2 * yg
    hsg = f64(hs)[:, unstriped(slot)]
    yh = mxq(f64(w2), 0, "e4m3").T @ xq
    hnew = 0.9 * hsg + 0.1 * ((yh) ** 2)
    ratio = mnew / (hnew + 0.2)
    return 0.95 * f64(par) - ((0.4 * (ratio - relu(ratio - 1.0) + relu(-1.0 * ratio - 1.0))) * np.sqrt(hnew))

@@ -1,0 +1,209 @@
+from contextlib import ExitStack
+
+import concourse.mybir as mybir
+from concourse.masks import make_identity
+
+K, T, S, N, U = 1024, 2048, 512, 256, 1024
+FLOPS = 2 * 2 * K * N * S
+
+F32 = mybir.dt.float32
+BF16 = mybir.dt.bfloat16
+I32 = mybir.dt.int32
+U32 = mybir.dt.uint32
+U16 = mybir.dt.uint16
+U8 = mybir.dt.uint8
+FP8X4 = mybir.dt.float8_e4m3fn_x4
+ALU = mybir.AluOpType
+ACT = mybir.ActivationFunctionType
+
+P = 128
+PACK = 4
+K_PASS = P * PACK
+PASSES = K // K_PASS
+BLOCKS = N // P
+CHUNKS = S // P
+HALF = S // 2
+
+
+def tile_picked_ysoph_par_p_kernel(tc, x_words, x_scales, w1, w2, ms, hs, par, offs, slot, out):
+    nc = tc.nc
+    with ExitStack() as ctx:
+        lists = ctx.enter_context(tc.tile_pool(name="lists", bufs=1))
+        keep = ctx.enter_context(tc.tile_pool(name="keep", bufs=1))
+        psum = ctx.enter_context(tc.psum_pool(name="psum", bufs=1))
+
+        def sb(name, shape, dtype):
+            return keep.tile(shape, dtype, name=name, align_bytes=64)
+
+        offs_sb = lists.tile([P, S // 16], U16, name="offs_sb")
+        slot_sb = lists.tile([P, S // 16], U16, name="slot_sb")
+
+        table_scales = sb("table_scales", [P, T], U8)
+        nc.gpsimd.memset(table_scales[:].bitcast(I32), 0)
+        seed = sb("seed", [P, 1], F32)
+        quarter = sb("quarter", [P, 1], F32)
+        nc.vector.memset(seed[:], 16.0)
+        nc.scalar.activation(quarter[:], seed[:], ACT.Abs_reciprocal_sqrt)
+        ident = sb("ident", [P, P], F32)
+        make_identity(nc, ident[:])
+
+        table_words = [sb(f"table_words{o}", [P, T], U32) for o in range(PASSES)]
+        picked_words = [sb(f"picked_words{o}", [P, S], U32) for o in range(PASSES)]
+        picked_scales = sb("picked_scales", [P, S], U8)
+
+        def load_words(o):
+            nc.sync.dma_start(table_words[o][:].bitcast(I32), x_words[o].rearrange("p c r -> p (c r)").bitcast(I32))
+
+        def load_scales():
+            for q in range(4):
+                nc.sync.dma_start(table_scales[32 * q : 32 * q + 8, :].bitcast(I32), x_scales[:, 4 * q : 4 * q + 4, :].bitcast(I32))
+
+        raw = {}
+
+        def load_w(name, w, o):
+            raw[name, o] = sb(f"raw_{name}{o}", [P, PACK, N], F32)
+            nc.sync.dma_start(raw[name, o][:], w[o * K_PASS : (o + 1) * K_PASS, :].rearrange("(p j) n -> p j n", j=PACK))
+
+        rows = {}
+
+        def load_rows(name, src, b):
+            rows[name, b] = sb(f"rows_{name}{b}", [P, src.shape[1]], F32)
+            nc.sync.dma_start(rows[name, b][:], src[b * P : (b + 1) * P, :])
+
+        nc.sync.dma_start(offs_sb[:], offs)
+        load_w("w2", w2, 0)
+        load_scales()
+        load_w("w2", w2, 1)
+        load_w("w1", w1, 0)
+        load_w("w1", w1, 1)
+        load_words(0)
+        load_words(1)
+        nc.sync.dma_start(slot_sb[:], slot)
+        load_rows("hs", hs, 0)
+        load_rows("ms", ms, 0)
+        load_rows("hs", hs, 1)
+        load_rows("ms", ms, 1)
+        load_rows("par", par, 0)
+        load_rows("par", par, 1)
+
+        codes, scales = {}, {}
+
+        def quantize(name, o, copy):
+            grouped = sb(f"grouped_{name}{o}", [P, N, PACK], BF16)
+            copy(grouped[:].rearrange("p (c i) t -> p c t i", i=4), raw[name, o][:].rearrange("p t (c i) -> p c t i", i=4))
+            codes[name, o] = sb(f"codes_{name}{o}", [P, N], U32)
+            scales[name, o] = sb(f"scales_{name}{o}", [P, N], U8)
+            nc.vector.quantize_mx(out=codes[name, o][:].bitcast(FP8X4), scales=scales[name, o][:], in_=grouped[:].rearrange("p n t -> p (n t)"))
+
+        acc = {}
+
+        def mx_pass(name, b, o):
+            if o == 0:
+                acc[name, b] = psum.tile([P, S], F32, name=f"acc_{name}{b}", tag=f"bank_{name}{b}")
+            cols = slice(b * P, (b + 1) * P)
+            nc.tensor.matmul_mx(
+                out=acc[name, b][:],
+                lhsT=codes[name, o][:, cols].bitcast(FP8X4),
+                lhsT_scale=scales[name, o][:, cols],
+                rhs=picked_words[o][:].bitcast(FP8X4),
+                rhs_scale=picked_scales[4 * o : P, :],
+                start=(o == 0),
+                stop=(o == PASSES - 1),
+            )
+
+        def work(name, b, width=S):
+            return sb(f"{name}{b}", [P, width], F32)
+
+        def pick_rows(name, b):
+            picked = work(f"picked_{name}", b)
+            nc.vector.tensor_copy(picked[:], rows[name, b][:].indirect(slot_sb[:]))
+            return picked
+
+        def turned_sum(name, b, first, second):
+            total = psum.tile([P, S], F32, name=f"sum_{name}{b}")
+            for c in range(CHUNKS):
+                cols = slice(c * P, (c + 1) * P)
+                nc.tensor.matmul(total[:, cols], lhsT=first[:, cols], rhs=ident[:], is_transpose=True, start=True, stop=False)
+                nc.tensor.matmul(total[:, cols], lhsT=second[:, cols], rhs=ident[:], is_transpose=True, start=False, stop=True)
+            return total
+
+        h, m, recip, root, sq, yq = {}, {}, {}, {}, {}, {}
+
+        def square(b):
+            sq[b] = work("sq", b)
+            nc.scalar.activation(sq[b][:], acc["w2", b][:], ACT.Square, scale=1.0 / 3.0)
+
+        def scaled(b):
+            yq[b] = work("yq", b)
+            nc.scalar.activation(yq[b][:], acc["w1", b][:], ACT.Copy, scale=0.25)
+
+        def curvature(b):
+            h[b] = turned_sum("h", b, pick_rows("hs", b), sq[b])
+
+        def momentum(b):
+            m[b] = turned_sum("m", b, pick_rows("ms", b), yq[b])
+
+        def factors(b):
+            rs = work("rs", b)
+            t1 = work("t1_", b)
+            recip[b] = work("recip", b)
+            root[b] = work("root", b)
+            nc.scalar.activation(rs[:], h[b][:], ACT.Abs_reciprocal_sqrt, bias=quarter[:], scale=1.125)
+            if b in (0,):
+                nc.scalar.activation(t1[:], h[b][:], ACT.Abs_reciprocal_sqrt, bias=2.0**-100)
+                nc.scalar.activation(recip[b][:], rs[:], ACT.Square)
+                nc.vector.scalar_tensor_tensor(root[b][:], h[b][:], 0.4 * 0.9**0.5, t1[:], ALU.mult, ALU.mult)
+            else:
+                t2 = work("t2_", b)
+                nc.scalar.activation(t1[:], h[b][:], ACT.Abs_reciprocal_sqrt, scale=0.9 * 0.16)
+                nc.scalar.activation(recip[b][:], rs[:], ACT.Square)
+                nc.scalar.activation(t2[:], t1[:], ACT.Square)
+                nc.scalar.activation(root[b][:], t2[:], ACT.Abs_reciprocal_sqrt)
+
+        def finish(b):
+            halves = [slice(u * HALF, (u + 1) * HALF) for u in range(2)]
+            ratio = [work(f"ratio{u}_", b, HALF) for u in range(2)]
+            clipped = [work(f"clipped{u}_", b, HALF) for u in range(2)]
+            step = [work(f"step{u}_", b, HALF) for u in range(2)]
+            res = [work(f"res{u}_", b, HALF) for u in range(2)]
+            for u in range(2):
+                nc.vector.tensor_tensor(ratio[u][:], m[b][:, halves[u]], recip[b][:, halves[u]], ALU.mult)
+            for u in range(2):
+                nc.vector.tensor_scalar(clipped[u][:], ratio[u][:], 1.0, -1.0, ALU.min, ALU.max)
+            for u in range(2):
+                nc.vector.tensor_tensor(step[u][:], clipped[u][:], root[b][:, halves[u]], ALU.mult)
+            for u in range(2):
+                back = psum.tile([P, HALF], F32, name=f"back{u}_{b}", tag=f"bank_{('w2', 'w1')[u]}{b}")
+                for c in range(CHUNKS // 2):
+                    cols = slice(c * P, (c + 1) * P)
+                    nc.tensor.transpose(back[:, cols], step[u][:, cols], ident[:])
+                nc.vector.scalar_tensor_tensor(res[u][:], rows["par", b][:, halves[u]], 0.95, back[:], ALU.mult, ALU.subtract)
+                nc.sync.dma_start(out[b * P : (b + 1) * P, halves[u]], res[u][:])
+
+        quantize("w2", 0, nc.scalar.copy)
+        nc.vector.tensor_copy(picked_scales[:], table_scales[:].indirect(offs_sb[:]))
+        quantize("w2", 1, nc.scalar.copy)
+        quantize("w1", 0, nc.scalar.copy)
+        quantize("w1", 1, nc.scalar.copy)
+        nc.vector.tensor_copy(picked_words[0][:], table_words[0][:].indirect(offs_sb[:]))
+        nc.vector.tensor_copy(picked_words[1][:], table_words[1][:].indirect(offs_sb[:]))
+        mx_pass("w2", 0, 0)
+        mx_pass("w1", 0, 0)
+        mx_pass("w2", 1, 0)
+        mx_pass("w1", 1, 0)
+        mx_pass("w2", 0, 1)
+        mx_pass("w1", 0, 1)
+        mx_pass("w2", 1, 1)
+        mx_pass("w1", 1, 1)
+        square(0)
+        scaled(0)
+        square(1)
+        scaled(1)
+        curvature(0)
+        momentum(0)
+        factors(0)
+        curvature(1)
+        momentum(1)
+        factors(1)
+        finish(0)
+        finish(1)

@@ -1,7 +1,6 @@
 from contextlib import ExitStack
 
 import concourse.mybir as mybir
-from concourse.masks import make_identity
 
 K, T, S, N, U = 1024, 2048, 512, 256, 1024
 FLOPS = 2 * 2 * K * N * S
@@ -32,8 +31,8 @@ def tile_picked_ysoph_par_p_kernel(tc, x_words, x_scales, w1, w2, ms, hs, par, o
         keep = ctx.enter_context(tc.tile_pool(name="keep", bufs=1))
         psum = ctx.enter_context(tc.psum_pool(name="psum", bufs=1))
 
-        def sb(name, shape, dtype):
-            return keep.tile(shape, dtype, name=name, align_bytes=64)
+        def sb(name, shape, dtype, tag=None):
+            return keep.tile(shape, dtype, name=name, tag=tag or name, align_bytes=64)
 
         offs_sb = lists.tile([P, S // 16], U16, name="offs_sb")
         slot_sb = lists.tile([P, S // 16], U16, name="slot_sb")
@@ -44,8 +43,6 @@ def tile_picked_ysoph_par_p_kernel(tc, x_words, x_scales, w1, w2, ms, hs, par, o
         quarter = sb("quarter", [P, 1], F32)
         nc.vector.memset(seed[:], 16.0)
         nc.scalar.activation(quarter[:], seed[:], ACT.Abs_reciprocal_sqrt)
-        ident = sb("ident", [P, P], F32)
-        make_identity(nc, ident[:])
 
         table_words = [sb(f"table_words{o}", [P, T], U32) for o in range(PASSES)]
         picked_words = [sb(f"picked_words{o}", [P, S], U32) for o in range(PASSES)]
@@ -74,136 +71,118 @@ def tile_picked_ysoph_par_p_kernel(tc, x_words, x_scales, w1, w2, ms, hs, par, o
         load_w("w2", w2, 0)
         load_scales()
         load_w("w2", w2, 1)
-        load_w("w1", w1, 0)
-        load_w("w1", w1, 1)
         load_words(0)
         load_words(1)
         nc.sync.dma_start(slot_sb[:], slot)
         load_rows("hs", hs, 0)
-        load_rows("ms", ms, 0)
         load_rows("hs", hs, 1)
-        load_rows("ms", ms, 1)
+        load_w("w1", w1, 0)
+        load_w("w1", w1, 1)
+        load_rows("ms", ms, 0)
         load_rows("par", par, 0)
+        load_rows("ms", ms, 1)
         load_rows("par", par, 1)
 
         codes, scales = {}, {}
 
-        def quantize(name, o, copy):
-            grouped = sb(f"grouped_{name}{o}", [P, N, PACK], BF16)
-            copy(grouped[:].rearrange("p (c i) t -> p c t i", i=4), raw[name, o][:].rearrange("p t (c i) -> p c t i", i=4))
-            codes[name, o] = sb(f"codes_{name}{o}", [P, N], U32)
-            scales[name, o] = sb(f"scales_{name}{o}", [P, N], U8)
-            nc.vector.quantize_mx(out=codes[name, o][:].bitcast(FP8X4), scales=scales[name, o][:], in_=grouped[:].rearrange("p n t -> p (n t)"))
+        def quantize(name, o, b, copy):
+            cols = slice(b * P, (b + 1) * P)
+            grouped = sb(f"grouped_{name}{o}{b}", [P, P, PACK], BF16)
+            copy(grouped[:].rearrange("p (c i) t -> p c t i", i=4), raw[name, o][:, :, cols].rearrange("p t (c i) -> p c t i", i=4))
+            codes[name, o, b] = sb(f"codes_{name}{o}{b}", [P, P], U32)
+            scales[name, o, b] = sb(f"scales_{name}{o}{b}", [P, P], U8)
+            nc.vector.quantize_mx(out=codes[name, o, b][:].bitcast(FP8X4), scales=scales[name, o, b][:], in_=grouped[:].rearrange("p n t -> p (n t)"))
 
         acc = {}
 
         def mx_pass(name, b, o):
             if o == 0:
-                acc[name, b] = psum.tile([P, S], F32, name=f"acc_{name}{b}", tag=f"bank_{name}{b}")
-            cols = slice(b * P, (b + 1) * P)
+                acc[name, b] = psum.tile([P, S], F32, name=f"acc_{name}{b}")
             nc.tensor.matmul_mx(
                 out=acc[name, b][:],
-                lhsT=codes[name, o][:, cols].bitcast(FP8X4),
-                lhsT_scale=scales[name, o][:, cols],
+                lhsT=codes[name, o, b][:].bitcast(FP8X4),
+                lhsT_scale=scales[name, o, b][:],
                 rhs=picked_words[o][:].bitcast(FP8X4),
                 rhs_scale=picked_scales[4 * o : P, :],
                 start=(o == 0),
                 stop=(o == PASSES - 1),
             )
 
+        def product(name, copies):
+            for b in range(BLOCKS):
+                for o in range(PASSES):
+                    quantize(name, o, b, copies[o][b])
+                for o in range(PASSES):
+                    mx_pass(name, b, o)
+
         def work(name, b, width=S):
             return sb(f"{name}{b}", [P, width], F32)
 
         def pick_rows(name, b):
-            picked = work(f"picked_{name}", b)
+            picked = sb(f"picked_{name}{b}", [P, S], F32, tag=f"grouped_w11{b}" if name == "ms" else None)
             nc.vector.tensor_copy(picked[:], rows[name, b][:].indirect(slot_sb[:]))
             return picked
 
-        def turned_sum(name, b, first, second):
-            total = psum.tile([P, S], F32, name=f"sum_{name}{b}")
-            for c in range(CHUNKS):
-                cols = slice(c * P, (c + 1) * P)
-                nc.tensor.matmul(total[:, cols], lhsT=first[:, cols], rhs=ident[:], is_transpose=True, start=True, stop=False)
-                nc.tensor.matmul(total[:, cols], lhsT=second[:, cols], rhs=ident[:], is_transpose=True, start=False, stop=True)
-            return total
+        h, recip, root = {}, {}, {}
 
-        h, m, recip, root, sq, yq = {}, {}, {}, {}, {}, {}
-
-        def square(b):
-            sq[b] = work("sq", b)
-            nc.scalar.activation(sq[b][:], acc["w2", b][:], ACT.Square, scale=1.0 / 3.0)
-
-        def scaled(b):
-            yq[b] = work("yq", b)
-            nc.scalar.activation(yq[b][:], acc["w1", b][:], ACT.Copy, scale=0.25)
-
-        def curvature(b):
-            h[b] = turned_sum("h", b, pick_rows("hs", b), sq[b])
-
-        def momentum(b):
-            m[b] = turned_sum("m", b, pick_rows("ms", b), yq[b])
+        def curvature(b, fused):
+            sq = work("sq", b)
+            nc.scalar.activation(sq[:], acc["w2", b][:], ACT.Square, scale=1.0 / 3.0)
+            h[b] = work("h", b)
+            if fused:
+                nc.vector.tensor_tensor(h[b][:], rows["hs", b][:].indirect(slot_sb[:]), sq[:], ALU.add)
+            else:
+                nc.vector.tensor_tensor(h[b][:], pick_rows("hs", b)[:], sq[:], ALU.add)
 
         def factors(b):
-            rs = work("rs", b)
-            t1 = work("t1_", b)
+            pair = sb(f"pair{b}", [P, 2, S], F32, tag="raw_w11")
+            rs, t1 = pair[:, 0, :], pair[:, 1, :]
             recip[b] = work("recip", b)
             root[b] = work("root", b)
-            nc.scalar.activation(rs[:], h[b][:], ACT.Abs_reciprocal_sqrt, bias=quarter[:], scale=1.125)
-            if b in (0,):
-                nc.scalar.activation(t1[:], h[b][:], ACT.Abs_reciprocal_sqrt, bias=2.0**-100)
-                nc.scalar.activation(recip[b][:], rs[:], ACT.Square)
-                nc.vector.scalar_tensor_tensor(root[b][:], h[b][:], 0.4 * 0.9**0.5, t1[:], ALU.mult, ALU.mult)
+            t2 = work("t2_", b)
+            nc.scalar.activation(rs, h[b][:], ACT.Abs_reciprocal_sqrt, bias=quarter[:], scale=1.125)
+            nc.scalar.activation(t1, h[b][:], ACT.Abs_reciprocal_sqrt, scale=0.9 * 0.16)
+            nc.scalar.activation(recip[b][:], rs, ACT.Square)
+            nc.scalar.activation(t2[:], t1, ACT.Square)
+            nc.scalar.activation(root[b][:], t2[:], ACT.Abs_reciprocal_sqrt)
+
+        def finish(b, pieces, fused):
+            width = S // pieces
+            parts = [slice(u * width, (u + 1) * width) for u in range(pieces)]
+            ratio = [work(f"ratio{u}_", b, width) for u in range(pieces)]
+            clipped = [work(f"clipped{u}_", b, width) for u in range(pieces)]
+            step = [work(f"step{u}_", b, width) for u in range(pieces)]
+            res = [work(f"res{u}_", b, width) for u in range(pieces)]
+            if fused:
+                yq = work("yq", b)
+                nc.scalar.activation(yq[:], acc["w1", b][:], ACT.Copy, scale=0.25)
+                whole = work("m", b)
+                nc.vector.tensor_tensor(whole[:], rows["ms", b][:].indirect(slot_sb[:]), yq[:], ALU.add)
+                m = [whole[:, parts[u]] for u in range(pieces)]
             else:
-                t2 = work("t2_", b)
-                nc.scalar.activation(t1[:], h[b][:], ACT.Abs_reciprocal_sqrt, scale=0.9 * 0.16)
-                nc.scalar.activation(recip[b][:], rs[:], ACT.Square)
-                nc.scalar.activation(t2[:], t1[:], ACT.Square)
-                nc.scalar.activation(root[b][:], t2[:], ACT.Abs_reciprocal_sqrt)
-
-        def finish(b):
-            halves = [slice(u * HALF, (u + 1) * HALF) for u in range(2)]
-            ratio = [work(f"ratio{u}_", b, HALF) for u in range(2)]
-            clipped = [work(f"clipped{u}_", b, HALF) for u in range(2)]
-            step = [work(f"step{u}_", b, HALF) for u in range(2)]
-            res = [work(f"res{u}_", b, HALF) for u in range(2)]
-            for u in range(2):
-                nc.vector.tensor_tensor(ratio[u][:], m[b][:, halves[u]], recip[b][:, halves[u]], ALU.mult)
-            for u in range(2):
+                picked = pick_rows("ms", b)
+                m = [work(f"m{u}_", b, width)[:] for u in range(pieces)]
+                for u in range(pieces):
+                    nc.vector.scalar_tensor_tensor(m[u], acc["w1", b][:, parts[u]], 0.25, picked[:, parts[u]], ALU.mult, ALU.add)
+            for u in range(pieces):
+                nc.vector.tensor_tensor(ratio[u][:], m[u], recip[b][:, parts[u]], ALU.mult)
+            for u in range(pieces):
                 nc.vector.tensor_scalar(clipped[u][:], ratio[u][:], 1.0, -1.0, ALU.min, ALU.max)
-            for u in range(2):
-                nc.vector.tensor_tensor(step[u][:], clipped[u][:], root[b][:, halves[u]], ALU.mult)
-            for u in range(2):
-                back = psum.tile([P, HALF], F32, name=f"back{u}_{b}", tag=f"bank_{('w2', 'w1')[u]}{b}")
-                for c in range(CHUNKS // 2):
-                    cols = slice(c * P, (c + 1) * P)
-                    nc.tensor.transpose(back[:, cols], step[u][:, cols], ident[:])
-                nc.vector.scalar_tensor_tensor(res[u][:], rows["par", b][:, halves[u]], 0.95, back[:], ALU.mult, ALU.subtract)
-                nc.sync.dma_start(out[b * P : (b + 1) * P, halves[u]], res[u][:])
+            for u in range(pieces):
+                nc.vector.tensor_tensor(step[u][:], clipped[u][:], root[b][:, parts[u]], ALU.mult)
+            for u in range(pieces):
+                nc.vector.scalar_tensor_tensor(res[u][:], rows["par", b][:, parts[u]], 0.95, step[u][:], ALU.mult, ALU.subtract)
+                nc.sync.dma_start(out[b * P : (b + 1) * P, parts[u]], res[u][:])
 
-        quantize("w2", 0, nc.scalar.copy)
-        nc.vector.tensor_copy(picked_scales[:], table_scales[:].indirect(offs_sb[:]))
-        quantize("w2", 1, nc.scalar.copy)
-        quantize("w1", 0, nc.scalar.copy)
-        quantize("w1", 1, nc.scalar.copy)
+        on_scalar = [[nc.scalar.copy] * BLOCKS] * PASSES
         nc.vector.tensor_copy(picked_words[0][:], table_words[0][:].indirect(offs_sb[:]))
+        nc.vector.tensor_copy(picked_scales[:], table_scales[:].indirect(offs_sb[:]))
         nc.vector.tensor_copy(picked_words[1][:], table_words[1][:].indirect(offs_sb[:]))
-        mx_pass("w2", 0, 0)
-        mx_pass("w1", 0, 0)
-        mx_pass("w2", 1, 0)
-        mx_pass("w1", 1, 0)
-        mx_pass("w2", 0, 1)
-        mx_pass("w1", 0, 1)
-        mx_pass("w2", 1, 1)
-        mx_pass("w1", 1, 1)
-        square(0)
-        scaled(0)
-        square(1)
-        scaled(1)
-        curvature(0)
-        momentum(0)
+        product("w2", on_scalar)
+        curvature(0, False)
+        product("w1", on_scalar)
+        curvature(1, False)
         factors(0)
-        curvature(1)
-        momentum(1)
         factors(1)
-        finish(0)
-        finish(1)
+        finish(0, 1, False)
+        finish(1, 2, False)

@@ -31,8 +31,8 @@ def tile_picked_ysoph_par_p_kernel(tc, x_words, x_scales, w1, w2, ms, hs, par, o
         keep = ctx.enter_context(tc.tile_pool(name="keep", bufs=1))
         psum = ctx.enter_context(tc.psum_pool(name="psum", bufs=1))
 
-        def sb(name, shape, dtype, tag=None):
-            return keep.tile(shape, dtype, name=name, tag=tag or name, align_bytes=64)
+        def sb(name, shape, dtype):
+            return keep.tile(shape, dtype, name=name, align_bytes=64)
 
         offs_sb = lists.tile([P, S // 16], U16, name="offs_sb")
         slot_sb = lists.tile([P, S // 16], U16, name="slot_sb")
@@ -68,19 +68,19 @@ def tile_picked_ysoph_par_p_kernel(tc, x_words, x_scales, w1, w2, ms, hs, par, o
             nc.sync.dma_start(rows[name, b][:], src[b * P : (b + 1) * P, :])
 
         nc.sync.dma_start(offs_sb[:], offs)
-        load_w("w2", w2, 0)
-        load_scales()
-        load_w("w2", w2, 1)
         load_words(0)
+        load_scales()
+        load_w("w2", w2, 0)
         load_words(1)
+        load_w("w2", w2, 1)
+        load_w("w1", w1, 0)
+        load_w("w1", w1, 1)
         nc.sync.dma_start(slot_sb[:], slot)
         load_rows("hs", hs, 0)
         load_rows("hs", hs, 1)
-        load_w("w1", w1, 0)
-        load_w("w1", w1, 1)
         load_rows("ms", ms, 0)
-        load_rows("par", par, 0)
         load_rows("ms", ms, 1)
+        load_rows("par", par, 0)
         load_rows("par", par, 1)
 
         codes, scales = {}, {}
@@ -108,81 +108,105 @@ def tile_picked_ysoph_par_p_kernel(tc, x_words, x_scales, w1, w2, ms, hs, par, o
                 stop=(o == PASSES - 1),
             )
 
-        def product(name, copies):
-            for b in range(BLOCKS):
-                for o in range(PASSES):
-                    quantize(name, o, b, copies[o][b])
-                for o in range(PASSES):
-                    mx_pass(name, b, o)
-
         def work(name, b, width=S):
             return sb(f"{name}{b}", [P, width], F32)
 
-        def pick_rows(name, b):
-            picked = sb(f"picked_{name}{b}", [P, S], F32, tag=f"grouped_w11{b}" if name == "ms" else None)
-            nc.vector.tensor_copy(picked[:], rows[name, b][:].indirect(slot_sb[:]))
-            return picked
+        t = {}
+        whole = [slice(0, S)]
+        halves = [slice(0, HALF), slice(HALF, S)]
 
-        h, recip, root = {}, {}, {}
+        def made(name, b):
+            t[name, b] = work(name, b)
+            return t[name, b]
 
-        def curvature(b, fused):
-            sq = work("sq", b)
-            nc.scalar.activation(sq[:], acc["w2", b][:], ACT.Square, scale=1.0 / 3.0)
-            h[b] = work("h", b)
-            if fused:
-                nc.vector.tensor_tensor(h[b][:], rows["hs", b][:].indirect(slot_sb[:]), sq[:], ALU.add)
-            else:
-                nc.vector.tensor_tensor(h[b][:], pick_rows("hs", b)[:], sq[:], ALU.add)
+        def act(name, b, source, func, parts=whole, **affine):
+            target = made(name, b)
+            for part in parts:
+                nc.scalar.activation(target[:, part], source[:, part], func, **affine)
 
-        def factors(b):
-            pair = sb(f"pair{b}", [P, 2, S], F32, tag="raw_w11")
-            rs, t1 = pair[:, 0, :], pair[:, 1, :]
-            recip[b] = work("recip", b)
-            root[b] = work("root", b)
-            t2 = work("t2_", b)
-            nc.scalar.activation(rs, h[b][:], ACT.Abs_reciprocal_sqrt, bias=quarter[:], scale=1.125)
-            nc.scalar.activation(t1, h[b][:], ACT.Abs_reciprocal_sqrt, scale=0.9 * 0.16)
-            nc.scalar.activation(recip[b][:], rs, ACT.Square)
-            nc.scalar.activation(t2[:], t1, ACT.Square)
-            nc.scalar.activation(root[b][:], t2[:], ACT.Abs_reciprocal_sqrt)
+        def square(b):
+            act("sq", b, acc["w2", b], ACT.Square, scale=1.0 / 3.0)
 
-        def finish(b, pieces, fused):
-            width = S // pieces
-            parts = [slice(u * width, (u + 1) * width) for u in range(pieces)]
-            ratio = [work(f"ratio{u}_", b, width) for u in range(pieces)]
-            clipped = [work(f"clipped{u}_", b, width) for u in range(pieces)]
-            step = [work(f"step{u}_", b, width) for u in range(pieces)]
-            res = [work(f"res{u}_", b, width) for u in range(pieces)]
-            if fused:
-                yq = work("yq", b)
-                nc.scalar.activation(yq[:], acc["w1", b][:], ACT.Copy, scale=0.25)
-                whole = work("m", b)
-                nc.vector.tensor_tensor(whole[:], rows["ms", b][:].indirect(slot_sb[:]), yq[:], ALU.add)
-                m = [whole[:, parts[u]] for u in range(pieces)]
-            else:
-                picked = pick_rows("ms", b)
-                m = [work(f"m{u}_", b, width)[:] for u in range(pieces)]
-                for u in range(pieces):
-                    nc.vector.scalar_tensor_tensor(m[u], acc["w1", b][:, parts[u]], 0.25, picked[:, parts[u]], ALU.mult, ALU.add)
-            for u in range(pieces):
-                nc.vector.tensor_tensor(ratio[u][:], m[u], recip[b][:, parts[u]], ALU.mult)
-            for u in range(pieces):
-                nc.vector.tensor_scalar(clipped[u][:], ratio[u][:], 1.0, -1.0, ALU.min, ALU.max)
-            for u in range(pieces):
-                nc.vector.tensor_tensor(step[u][:], clipped[u][:], root[b][:, parts[u]], ALU.mult)
-            for u in range(pieces):
-                nc.vector.scalar_tensor_tensor(res[u][:], rows["par", b][:, parts[u]], 0.95, step[u][:], ALU.mult, ALU.subtract)
-                nc.sync.dma_start(out[b * P : (b + 1) * P, parts[u]], res[u][:])
+        def scaled(b):
+            act("yq", b, acc["w1", b], ACT.Copy, scale=0.25)
 
-        on_scalar = [[nc.scalar.copy] * BLOCKS] * PASSES
+        def curvature(b):
+            nc.vector.tensor_tensor(made("h", b)[:], rows["hs", b][:].indirect(slot_sb[:]), t["sq", b][:], ALU.add)
+
+        def momentum(b):
+            nc.vector.tensor_tensor(made("m", b)[:], rows["ms", b][:].indirect(slot_sb[:]), t["yq", b][:], ALU.add)
+
+        def inverse_roots(b):
+            act("rs", b, t["h", b], ACT.Abs_reciprocal_sqrt, bias=quarter[:], scale=1.125)
+            act("ri", b, t["h", b], ACT.Abs_reciprocal_sqrt, scale=0.9 * 0.16)
+
+        def recip(b):
+            act("recip", b, t["rs", b], ACT.Square)
+
+        def inverse(b, parts=whole):
+            act("inv", b, t["ri", b], ACT.Square, parts)
+
+        def root(b, parts=whole):
+            act("root", b, t["inv", b], ACT.Abs_reciprocal_sqrt, parts)
+
+        def ratio(b):
+            nc.vector.tensor_tensor(made("ratio", b)[:], t["m", b][:], t["recip", b][:], ALU.mult)
+
+        def clip(b):
+            nc.vector.tensor_scalar(made("clipped", b)[:], t["ratio", b][:], 1.0, -1.0, ALU.min, ALU.max)
+
+        def step(b, parts=whole):
+            target = made("step", b)
+            for part in parts:
+                nc.vector.tensor_tensor(target[:, part], t["clipped", b][:, part], t["root", b][:, part], ALU.mult)
+
+        def update(b, parts=whole):
+            target = made("res", b)
+            for part in parts:
+                nc.vector.scalar_tensor_tensor(target[:, part], rows["par", b][:, part], 0.95, t["step", b][:, part], ALU.mult, ALU.subtract)
+                nc.sync.dma_start(out[b * P : (b + 1) * P, part], target[:, part])
+
+        on_scalar, on_vector = nc.scalar.copy, nc.vector.tensor_copy
         nc.vector.tensor_copy(picked_words[0][:], table_words[0][:].indirect(offs_sb[:]))
         nc.vector.tensor_copy(picked_scales[:], table_scales[:].indirect(offs_sb[:]))
         nc.vector.tensor_copy(picked_words[1][:], table_words[1][:].indirect(offs_sb[:]))
-        product("w2", on_scalar)
-        curvature(0, False)
-        product("w1", on_scalar)
-        curvature(1, False)
-        factors(0)
-        factors(1)
-        finish(0, 1, False)
-        finish(1, 2, False)
+        quantize("w2", 0, 0, on_scalar)
+        quantize("w2", 0, 1, on_scalar)
+        quantize("w2", 1, 0, on_vector)
+        quantize("w2", 1, 1, on_scalar)
+        mx_pass("w2", 0, 0)
+        mx_pass("w2", 1, 0)
+        mx_pass("w2", 0, 1)
+        mx_pass("w2", 1, 1)
+        square(0)
+        quantize("w1", 0, 0, on_vector)
+        quantize("w1", 0, 1, on_scalar)
+        quantize("w1", 1, 0, on_vector)
+        quantize("w1", 1, 1, on_scalar)
+        mx_pass("w1", 0, 0)
+        mx_pass("w1", 0, 1)
+        mx_pass("w1", 1, 0)
+        mx_pass("w1", 1, 1)
+        square(1)
+        curvature(0)
+        scaled(0)
+        curvature(1)
+        inverse_roots(0)
+        scaled(1)
+        momentum(0)
+        recip(0)
+        inverse(0)
+        inverse_roots(1)
+        momentum(1)
+        recip(1)
+        root(0)
+        inverse(1, halves)
+        root(1, halves)
+        ratio(0)
+        clip(0)
+        ratio(1)
+        step(0)
+        clip(1)
+        update(0)
+        step(1, halves)
+        update(1, halves)

from contextlib import ExitStack

import concourse.mybir as mybir

K, T, S, N, U = 1024, 2048, 512, 256, 1024
FLOPS = 2 * 2 * K * N * S

F32 = mybir.dt.float32
BF16 = mybir.dt.bfloat16
I32 = mybir.dt.int32
U32 = mybir.dt.uint32
U16 = mybir.dt.uint16
U8 = mybir.dt.uint8
FP8X4 = mybir.dt.float8_e4m3fn_x4
ALU = mybir.AluOpType
ACT = mybir.ActivationFunctionType

P = 128
PACK = 4
K_PASS = P * PACK
PASSES = K // K_PASS
BLOCKS = N // P
CHUNKS = S // P
HALF = S // 2


def tile_picked_ysoph_par_p_kernel(tc, x_words, x_scales, w1, w2, ms, hs, par, offs, slot, out):
    nc = tc.nc
    with ExitStack() as ctx:
        lists = ctx.enter_context(tc.tile_pool(name="lists", bufs=1))
        keep = ctx.enter_context(tc.tile_pool(name="keep", bufs=1))
        psum = ctx.enter_context(tc.psum_pool(name="psum", bufs=1))

        def sb(name, shape, dtype):
            return keep.tile(shape, dtype, name=name, align_bytes=64)

        offs_sb = lists.tile([P, S // 16], U16, name="offs_sb")
        slot_sb = lists.tile([P, S // 16], U16, name="slot_sb")

        table_scales = sb("table_scales", [P, T], U8)
        nc.gpsimd.memset(table_scales[:].bitcast(I32), 0)
        seed = sb("seed", [P, 1], F32)
        quarter = sb("quarter", [P, 1], F32)
        nc.vector.memset(seed[:], 16.0)
        nc.scalar.activation(quarter[:], seed[:], ACT.Abs_reciprocal_sqrt)

        table_words = [sb(f"table_words{o}", [P, T], U32) for o in range(PASSES)]
        picked_words = [sb(f"picked_words{o}", [P, S], U32) for o in range(PASSES)]
        picked_scales = sb("picked_scales", [P, S], U8)

        def load_words(o):
            nc.sync.dma_start(table_words[o][:].bitcast(I32), x_words[o].rearrange("p c r -> p (c r)").bitcast(I32))

        def load_scales():
            for q in range(4):
                nc.sync.dma_start(table_scales[32 * q : 32 * q + 8, :].bitcast(I32), x_scales[:, 4 * q : 4 * q + 4, :].bitcast(I32))

        raw = {}

        def load_w(name, w, o):
            raw[name, o] = sb(f"raw_{name}{o}", [P, PACK, N], F32)
            nc.sync.dma_start(raw[name, o][:], w[o * K_PASS : (o + 1) * K_PASS, :].rearrange("(p j) n -> p j n", j=PACK))

        rows = {}

        def load_rows(name, src, b):
            rows[name, b] = sb(f"rows_{name}{b}", [P, src.shape[1]], F32)
            nc.sync.dma_start(rows[name, b][:], src[b * P : (b + 1) * P, :])

        nc.sync.dma_start(offs_sb[:], offs)
        load_words(0)
        load_scales()
        load_w("w2", w2, 0)
        load_words(1)
        load_w("w2", w2, 1)
        load_w("w1", w1, 0)
        load_w("w1", w1, 1)
        nc.sync.dma_start(slot_sb[:], slot)
        load_rows("hs", hs, 0)
        load_rows("hs", hs, 1)
        load_rows("ms", ms, 0)
        load_rows("ms", ms, 1)
        load_rows("par", par, 0)
        load_rows("par", par, 1)

        codes, scales = {}, {}

        def quantize(name, o, b, copy):
            cols = slice(b * P, (b + 1) * P)
            grouped = sb(f"grouped_{name}{o}{b}", [P, P, PACK], BF16)
            copy(grouped[:].rearrange("p (c i) t -> p c t i", i=4), raw[name, o][:, :, cols].rearrange("p t (c i) -> p c t i", i=4))
            codes[name, o, b] = sb(f"codes_{name}{o}{b}", [P, P], U32)
            scales[name, o, b] = sb(f"scales_{name}{o}{b}", [P, P], U8)
            nc.vector.quantize_mx(out=codes[name, o, b][:].bitcast(FP8X4), scales=scales[name, o, b][:], in_=grouped[:].rearrange("p n t -> p (n t)"))

        acc = {}

        def mx_pass(name, b, o):
            if o == 0:
                acc[name, b] = psum.tile([P, S], F32, name=f"acc_{name}{b}")
            nc.tensor.matmul_mx(
                out=acc[name, b][:],
                lhsT=codes[name, o, b][:].bitcast(FP8X4),
                lhsT_scale=scales[name, o, b][:],
                rhs=picked_words[o][:].bitcast(FP8X4),
                rhs_scale=picked_scales[4 * o : P, :],
                start=(o == 0),
                stop=(o == PASSES - 1),
            )

        def work(name, b, width=S):
            return sb(f"{name}{b}", [P, width], F32)

        t = {}
        whole = [slice(0, S)]
        halves = [slice(0, HALF), slice(HALF, S)]

        def made(name, b):
            t[name, b] = work(name, b)
            return t[name, b]

        def act(name, b, source, func, parts=whole, **affine):
            target = made(name, b)
            for part in parts:
                nc.scalar.activation(target[:, part], source[:, part], func, **affine)

        def square(b):
            act("sq", b, acc["w2", b], ACT.Square, scale=1.0 / 3.0)

        def scaled(b):
            act("yq", b, acc["w1", b], ACT.Copy, scale=0.25)

        def curvature(b):
            nc.vector.tensor_tensor(made("h", b)[:], rows["hs", b][:].indirect(slot_sb[:]), t["sq", b][:], ALU.add)

        def momentum(b):
            nc.vector.tensor_tensor(made("m", b)[:], rows["ms", b][:].indirect(slot_sb[:]), t["yq", b][:], ALU.add)

        def inverse_roots(b):
            act("rs", b, t["h", b], ACT.Abs_reciprocal_sqrt, bias=quarter[:], scale=1.125)
            act("ri", b, t["h", b], ACT.Abs_reciprocal_sqrt, scale=0.9 * 0.16)

        def recip(b):
            act("recip", b, t["rs", b], ACT.Square)

        def inverse(b, parts=whole):
            act("inv", b, t["ri", b], ACT.Square, parts)

        def root(b, parts=whole):
            act("root", b, t["inv", b], ACT.Abs_reciprocal_sqrt, parts)

        def ratio(b):
            nc.vector.tensor_tensor(made("ratio", b)[:], t["m", b][:], t["recip", b][:], ALU.mult)

        def clip(b):
            nc.vector.tensor_scalar(made("clipped", b)[:], t["ratio", b][:], 1.0, -1.0, ALU.min, ALU.max)

        def step(b, parts=whole):
            target = made("step", b)
            for part in parts:
                nc.vector.tensor_tensor(target[:, part], t["clipped", b][:, part], t["root", b][:, part], ALU.mult)

        def update(b, parts=whole):
            target = made("res", b)
            for part in parts:
                nc.vector.scalar_tensor_tensor(target[:, part], rows["par", b][:, part], 0.95, t["step", b][:, part], ALU.mult, ALU.subtract)
                nc.sync.dma_start(out[b * P : (b + 1) * P, part], target[:, part])

        on_scalar, on_vector = nc.scalar.copy, nc.vector.tensor_copy
        nc.vector.tensor_copy(picked_words[0][:], table_words[0][:].indirect(offs_sb[:]))
        nc.vector.tensor_copy(picked_scales[:], table_scales[:].indirect(offs_sb[:]))
        nc.vector.tensor_copy(picked_words[1][:], table_words[1][:].indirect(offs_sb[:]))
        quantize("w2", 0, 0, on_scalar)
        quantize("w2", 0, 1, on_scalar)
        quantize("w2", 1, 0, on_vector)
        quantize("w2", 1, 1, on_scalar)
        mx_pass("w2", 0, 0)
        mx_pass("w2", 1, 0)
        mx_pass("w2", 0, 1)
        mx_pass("w2", 1, 1)
        square(0)
        quantize("w1", 0, 0, on_vector)
        quantize("w1", 0, 1, on_scalar)
        quantize("w1", 1, 0, on_vector)
        quantize("w1", 1, 1, on_scalar)
        mx_pass("w1", 0, 0)
        mx_pass("w1", 0, 1)
        mx_pass("w1", 1, 0)
        mx_pass("w1", 1, 1)
        square(1)
        curvature(0)
        scaled(0)
        curvature(1)
        inverse_roots(0)
        scaled(1)
        momentum(0)
        recip(0)
        inverse(0)
        inverse_roots(1)
        momentum(1)
        recip(1)
        root(0)
        inverse(1, halves)
        root(1, halves)
        ratio(0)
        clip(0)
        ratio(1)
        step(0)
        clip(1)
        update(0)
        step(1, halves)
        update(1, halves)
